import numpy as np, ml_dtypes
CORES = [12,28,60,100,156,228]
N = 6
TOK, K = 64, 3
EPS = 0.01
ROUTE = [[[0,2,5],[2,3,5],[0,2,5],[1,3,5],[0,3,5],[1,3,4],[3,4,5],[0,2,4],[1,3,4],[0,3,4],[3,4,5],[1,3,4],[2,3,4],[0,2,5],[2,3,4],[0,2,4],[0,1,2],[3,4,5],[1,2,4],[1,2,5],[0,1,4],[1,2,4],[1,2,5],[1,2,5],[0,2,3],[2,4,5],[0,1,4],[0,4,5],[0,1,3],[1,2,4],[3,4,5],[1,3,4],[0,3,5],[2,3,4],[0,2,3],[0,1,5],[0,2,3],[0,2,5],[0,4,5],[0,3,4],[1,3,4],[0,3,4],[1,3,5],[0,2,3],[2,3,5],[1,2,5],[2,3,5],[0,2,4],[0,1,2],[0,1,2],[0,2,5],[0,1,2],[0,4,5],[1,3,5],[1,2,3],[0,1,3],[1,2,5],[1,4,5],[0,3,4],[1,4,5],[1,2,4],[0,3,5],[0,3,5],[1,3,5]],[[1,2,5],[0,3,4],[1,2,5],[2,3,5],[2,3,4],[1,2,4],[2,3,4],[0,2,3],[2,4,5],[0,1,5],[1,4,5],[0,1,4],[1,3,4],[0,2,3],[0,2,5],[1,3,4],[2,3,4],[1,3,5],[1,2,3],[2,4,5],[2,3,5],[2,3,4],[2,3,5],[2,3,4],[1,3,4],[2,3,4],[3,4,5],[0,3,5],[0,2,5],[2,4,5],[1,2,5],[3,4,5],[1,2,4],[2,3,5],[0,2,5],[0,1,3],[1,4,5],[2,4,5],[0,2,5],[1,3,5],[1,3,5],[0,1,4],[0,1,5],[0,4,5],[0,1,5],[0,2,3],[0,2,3],[0,2,4],[0,4,5],[1,2,5],[2,4,5],[0,1,4],[1,4,5],[1,2,5],[0,2,5],[1,2,3],[0,1,3],[0,1,5],[1,4,5],[0,3,5],[2,3,5],[2,3,4],[0,3,4],[0,2,4]],[[3,4,5],[2,4,5],[0,4,5],[0,4,5],[1,3,5],[0,2,4],[3,4,5],[0,1,2],[1,3,4],[3,4,5],[0,4,5],[1,2,5],[0,1,3],[0,1,4],[2,3,4],[0,1,5],[0,2,3],[0,4,5],[2,3,5],[2,3,4],[1,4,5],[0,2,3],[0,4,5],[0,4,5],[1,3,4],[1,2,4],[0,3,5],[0,1,2],[1,2,5],[2,3,5],[2,3,4],[0,1,4],[1,3,4],[1,3,4],[0,1,4],[3,4,5],[0,4,5],[3,4,5],[1,2,5],[0,1,2],[0,2,3],[1,4,5],[1,2,4],[2,3,4],[0,2,3],[2,4,5],[1,3,4],[0,1,4],[1,2,4],[1,2,3],[0,1,3],[0,4,5],[1,4,5],[1,2,3],[2,3,5],[1,2,3],[1,2,5],[0,1,4],[1,3,4],[0,2,5],[0,2,5],[0,1,4],[0,1,5],[2,4,5]],[[2,4,5],[1,3,4],[2,3,4],[1,2,3],[1,3,5],[1,2,5],[0,4,5],[0,2,4],[3,4,5],[1,3,4],[2,3,4],[0,3,5],[2,3,4],[0,1,4],[0,4,5],[1,4,5],[2,4,5],[0,2,5],[1,3,5],[0,3,4],[2,3,5],[1,2,4],[0,4,5],[2,3,5],[3,4,5],[1,3,5],[0,1,4],[0,3,5],[0,1,2],[1,2,5],[1,2,4],[1,3,4],[0,2,5],[1,3,4],[0,1,2],[0,1,2],[2,3,5],[1,3,4],[2,4,5],[0,2,5],[1,3,5],[0,3,5],[0,2,5],[1,2,3],[3,4,5],[1,2,4],[1,2,5],[0,1,3],[0,4,5],[0,2,4],[0,3,4],[1,4,5],[0,2,4],[2,4,5],[0,2,4],[0,4,5],[1,2,5],[0,1,3],[1,2,3],[2,3,4],[0,2,4],[0,2,4],[0,3,5],[2,3,4]],[[0,1,2],[2,4,5],[0,1,2],[3,4,5],[1,3,4],[1,4,5],[1,2,3],[2,3,5],[0,1,4],[1,2,5],[0,3,4],[0,4,5],[1,3,5],[1,4,5],[0,3,5],[0,3,4],[2,3,4],[0,4,5],[1,3,5],[0,4,5],[0,2,3],[2,4,5],[0,1,3],[1,2,4],[0,3,4],[1,2,4],[0,2,3],[2,3,5],[1,3,5],[2,4,5],[2,3,4],[0,1,4],[0,1,5],[2,3,5],[0,1,2],[0,3,5],[2,3,4],[3,4,5],[1,3,4],[0,1,5],[1,3,4],[1,3,5],[2,3,5],[3,4,5],[1,3,4],[1,4,5],[1,3,4],[1,4,5],[1,2,5],[0,2,4],[0,1,5],[0,1,4],[0,1,2],[0,3,5],[1,3,4],[0,2,4],[0,1,4],[0,1,3],[0,1,3],[0,3,4],[0,1,2],[0,2,3],[0,1,2],[1,3,4]],[[2,3,4],[0,2,3],[1,2,5],[0,4,5],[1,2,5],[2,4,5],[1,2,3],[1,2,5],[1,3,4],[2,3,5],[2,3,4],[0,2,4],[2,4,5],[0,1,3],[3,4,5],[1,4,5],[0,3,4],[1,4,5],[1,3,4],[0,3,4],[0,4,5],[0,2,5],[0,1,5],[0,1,4],[0,4,5],[0,3,5],[3,4,5],[2,3,4],[0,1,4],[2,4,5],[2,3,5],[0,2,5],[1,3,5],[1,3,5],[0,2,5],[1,3,5],[1,4,5],[1,3,4],[0,4,5],[2,4,5],[1,3,5],[1,3,4],[1,2,5],[0,2,3],[3,4,5],[0,1,4],[1,2,3],[0,1,3],[0,1,3],[1,4,5],[1,4,5],[0,2,3],[0,1,4],[0,2,3],[0,1,4],[2,3,4],[0,2,4],[0,3,4],[0,1,3],[0,1,3],[2,4,5],[1,3,5],[0,3,4],[0,4,5]]]
def sigmoid(z):
    a = np.exp(-np.abs(z)); return np.where(z >= 0, 1.0, a) / (1.0 + a)
def setup_inputs(rng):
    rt = (0.75 * rng.standard_normal((128, 1), dtype=np.float32) + rng.standard_normal((128, N), dtype=np.float32) / 2).astype(ml_dtypes.bfloat16)
    rm = np.zeros((N, N, TOK), np.float32)
    for r in range(N):
        for t in range(TOK): rm[r, ROUTE[r][t], t] = 1.0
    return {"x": (rng.standard_normal((N, 128, TOK), dtype=np.float32) / 8).astype(ml_dtypes.bfloat16), "rt": np.broadcast_to(rt, (N, 128, N)).copy(), "rm": rm.astype(ml_dtypes.bfloat16), "w": rng.standard_normal((N, 128, 128), dtype=np.float32).astype(ml_dtypes.bfloat16)}
def setup_inputs_big(rng):
    d = setup_inputs(rng)
    for k in ("x", "w"): d[k] = (d[k].astype(np.float32) * 1024.0).astype(d[k].dtype)
    return d
def setup_inputs_small(rng):
    d = setup_inputs(rng)
    for k in ("x", "w"): d[k] = (d[k].astype(np.float32) * (1 / 1024.0)).astype(d[k].dtype)
    return d
def setup_inputs_apart(rng):
    d = setup_inputs(rng)
    f = (10.0 ** rng.permutation(np.linspace(-1.5, 1.5, N))).astype(np.float32).reshape(N, 1, 1)
    for k in ("x",): d[k] = (d[k].astype(np.float32) * f).astype(d[k].dtype)
    return d
def setup_inputs_faint(rng):
    d = setup_inputs(rng); x = d["x"].astype(np.float32); rt = d["rt"][0].astype(np.float32); t = int(rng.integers(N))
    p = rt @ np.linalg.solve(rt.T @ rt, np.ones(N, np.float32))
    x[t] = x[t] / 16 - np.outer(p, rng.uniform(20, 22, TOK).astype(np.float32))
    d["x"] = x.astype(d["x"].dtype)
    return d
def reference(x, rt, rm, w):
    X, RT, W = x.astype(np.float64), rt.astype(np.float64), w.astype(np.float64)
    y = np.zeros((N, 128, TOK))
    for r in range(N):
        sc = RT[r].T @ X[r]
        for t in range(TOK):
            ex = ROUTE[r][t]; g = sigmoid(sc[ex, t]); g = g / (g.sum() + EPS)
            y[r][:, t] = sum(g[i] * (W[e].T @ X[r][:, t]) for i, e in enumerate(ex))
    return {"y": y.astype(ml_dtypes.bfloat16)}

from concourse.bass import DstId, RemoteDMATransfer
from concourse.mybir import AluOpType, ActivationFunctionType

NR, DIM, TOK = 6, 128, 64
EPS = 0.01
SIM_CORES = 256

SCRATCH = {
    "wd": ("dram", [DIM, DIM], "bfloat16"),
    "wS": ("sbuf", [DIM, NR * DIM], "bfloat16"),
    "xS": ("sbuf", [DIM, TOK], "bfloat16"),
    "rtS": ("sbuf", [DIM, NR], "bfloat16"),
    "rmS": ("sbuf", [DIM, TOK], "bfloat16"),
    "pidx": ("sbuf", [DIM, DIM], "bfloat16"),
    "ones": ("sbuf", [DIM, DIM], "bfloat16"),
    "sel": ("sbuf", [DIM, NR * DIM], "bfloat16"),
    "aS": ("sbuf", [DIM, TOK], "float32"),
    "am": ("sbuf", [DIM, TOK], "bfloat16"),
    "den": ("sbuf", [DIM, TOK], "float32"),
    "rec": ("sbuf", [DIM, TOK], "float32"),
    "xr": ("sbuf", [DIM, TOK], "float32"),
    "xg": ("sbuf", [DIM, NR * TOK], "bfloat16"),
    "yS": ("sbuf", [DIM, TOK], "bfloat16"),
    "ps_s": ("psum", [DIM, 512], "float32"),
    "ps_d": ("psum", [DIM, 512], "float32"),
    "ps_ab": ("psum", [DIM, 512], "float32"),
    "ps_y": ("psum", [DIM, 512], "float32"),
}
SEMAPHORES = ["wd", "wo", "xr", "rm", "pn", "sel", "s", "a", "am", "d", "ab", "v1", "v2", "v3", "xg", "mm", "o", "st",
              "rl", "ls"] + ["arr%d" % e for e in range(NR)]


def _bits(m):
    return [i for i in range(m.bit_length()) if (m >> i) & 1]


def _mask(engines):
    return sum(1 << i for i in engines)


def _relays(cores, topo):
    used, load, relay = set(cores), {}, {}
    for s, cs in enumerate(cores):
        mates = [k for k in range(SIM_CORES) if topo.host(k) == topo.host(cs) and topo.chip(k) == topo.chip(cs)]
        for d, cd in enumerate(cores):
            if s == d or topo.may_write(cs, cd):
                continue
            cand = [k for k in mates if k not in used and topo.may_write(k, cd)]
            k = min(cand, key=lambda k: (load.get(("in", d, topo.die(k)), 0) + load.get(("out", s, topo.die(k)), 0),
                                         topo.die(k) != topo.die(cs), k))
            used.add(k)
            relay[(s, d)] = k
            for key in (("in", d, topo.die(k)), ("out", s, topo.die(k))):
                load[key] = load.get(key, 0) + 1
    return relay


def _dst(topo, dst, src):
    rid, pid = topo.addr(dst, src)
    return DstId(rid=rid, pnc=pid)


def rank_program(g, core, T, topo):
    cores = list(T.cores)
    relay = _relays(cores, topo)
    sem = T.sem
    rank = T.rank_of(core)

    def block(e):
        return T.wS[:, e * DIM:(e + 1) * DIM]

    def hand_engines(s):
        helpers = [relay[(s, d)] for d in range(NR) if (s, d) in relay]
        off = 0
        for d in range(NR):
            if d != s and topo.may_write(cores[s], cores[d]):
                off |= topo.mask(cores[s], cores[d])
        free = _bits(topo.mask(cores[s], helpers[0]) & ~off)
        per = 1
        while per * 2 * len(helpers) <= len(free):
            per *= 2
        return {k: free[i * per:(i + 1) * per] for i, k in enumerate(helpers)}

    if rank is None:
        for (s, d), k in relay.items():
            if k != core:
                continue
            m = topo.mask(core, cores[d])
            rid, pid = topo.addr(cores[d], core)
            g.wait_ge(sem.rl, len(hand_engines(s)[core]))
            g.remote_dma(block(s), T.wd[:], sem["arr%d" % s], sem.ls, pid, rid, m)
            g.wait_ge(sem.ls, len(_bits(m)))
        return

    r = rank
    direct = sorted((d for d in range(NR) if d != r and (r, d) not in relay), key=lambda d: (d - r) % NR)

    g.sync.dma_start(T.wd[:], T.w[:]).then_inc(sem.wd, 16)
    g.scalar.dma_start(T.xS[:], T.x[:]).then_inc(sem.xr, 16)
    g.sync.dma_start(T.rtS[:], T.rt[:]).then_inc(sem.xr, 16)
    g.scalar.dma_start(T.rmS[0:NR, :], T.rm[:]).then_inc(sem.rm, 16)
    g.sync.dma_start(block(r), T.w[:]).then_inc(sem.wo, 16)

    g.iota(T.pidx[0:NR, :], [[0, DIM]], 0, 1, allow_small_or_imprecise_dtypes=True).then_inc(sem.pn, 1)
    g.wait_ge(sem.wd, 16)
    hand = hand_engines(r)
    g.remote_dma_fused(
        [RemoteDMATransfer(dst_ids=[_dst(topo, k, core)], dma_engine_mask=_mask(eng), remote_sem=sem.rl,
                           src=T.wd[:], dst=T.wd[:]) for k, eng in hand.items()],
        local_sem=sem.ls)
    sent = sum(len(eng) for eng in hand.values())
    off = topo.mask(core, cores[direct[0]])
    g.remote_dma_fused(
        [RemoteDMATransfer(dst_ids=[_dst(topo, cores[d], core) for d in direct], dma_engine_mask=off,
                           remote_sem=sem["arr%d" % r], srcs=[T.wd[:]], dsts=[block(r) for d in direct])],
        local_sem=sem.ls)
    sent += len(_bits(off))

    v, pe, act = g.vector, g.tensor, g.scalar
    v.memset(T.ones[0:NR, :], 1.0).then_inc(sem.sel, 1)
    v.wait_ge(sem.pn, 1)
    for e in range(NR):
        v.tensor_scalar(T.sel[0:NR, e * DIM:(e + 1) * DIM], T.pidx[0:NR, :], float(e), None,
                        AluOpType.is_equal).then_inc(sem.sel, 1)

    pe.wait_ge(sem.xr, 32)
    pe.matmul(T.ps_s[0:NR, 0:TOK], T.rtS[:], T.xS[:], True, True).then_inc(sem.s, 1)
    act.wait_ge(sem.s, 1)
    act.activation(T.aS[0:NR, :], T.ps_s[0:NR, 0:TOK], ActivationFunctionType.Sigmoid).then_inc(sem.a, 1)
    v.wait_ge(sem.a, 1)
    v.wait_ge(sem.rm, 16)
    v.tensor_tensor(T.am[0:NR, :], T.aS[0:NR, :], T.rmS[0:NR, :], AluOpType.mult).then_inc(sem.am, 1)

    pe.wait_ge(sem.am, 1)
    pe.wait_ge(sem.sel, NR + 1)
    pe.matmul(T.ps_d[:, 0:TOK], T.ones[0:NR, :], T.am[0:NR, :], True, True).then_inc(sem.d, 1)
    for e in range(NR):
        pe.matmul(T.ps_ab[:, e * TOK:(e + 1) * TOK], T.sel[0:NR, e * DIM:(e + 1) * DIM], T.am[0:NR, :],
                  True, True).then_inc(sem.ab, 1)

    v.wait_ge(sem.d, 1)
    v.tensor_scalar(T.den[:], T.ps_d[:, 0:TOK], EPS, None, AluOpType.add).then_inc(sem.v1, 1)
    v.wait_ge(sem.v1, 1)
    v.reciprocal(T.rec[:], T.den[:]).then_inc(sem.v2, 1)
    v.wait_ge(sem.v2, 1)
    v.wait_ge(sem.xr, 32)
    v.tensor_tensor(T.xr[:], T.xS[:], T.rec[:], AluOpType.mult).then_inc(sem.v3, 1)
    v.wait_ge(sem.v3, 1)
    v.wait_ge(sem.ab, NR)
    for e in range(NR):
        v.tensor_tensor(T.xg[:, e * TOK:(e + 1) * TOK], T.ps_ab[:, e * TOK:(e + 1) * TOK], T.xr[:],
                        AluOpType.mult).then_inc(sem.xg, 1)

    order = [r] + sorted((s for s in range(NR) if s != r and (s, r) not in relay), key=lambda s: (r - s) % NR) \
        + [s for s in range(NR) if (s, r) in relay]
    pe.wait_ge(sem.xg, NR)
    for i, s in enumerate(order):
        if s == r:
            pe.wait_ge(sem.wo, 16)
        else:
            src = relay.get((s, r), cores[s])
            pe.wait_ge(sem["arr%d" % s], len(_bits(topo.mask(src, core))))
        pe.matmul(T.ps_y[:, 0:TOK], block(s), T.xg[:, s * TOK:(s + 1) * TOK], i == 0,
                  i == NR - 1).then_inc(sem.mm, 1)
    v.wait_ge(sem.mm, NR)
    v.tensor_copy(T.yS[:], T.ps_y[:, 0:TOK]).then_inc(sem.o, 1)
    g.sync.wait_ge(sem.o, 1)
    g.sync.dma_start(T.y[:], T.yS[:]).then_inc(sem.st, 16)
    g.sync.wait_ge(sem.st, 16)
    g.wait_ge(sem.ls, sent)
